import numpy as np
import ml_dtypes


def mxq(x, axis, fmt="e4m3"):
    dtype, down = {"e4m3": (ml_dtypes.float8_e4m3fn, 7), "e5m2": (ml_dtypes.float8_e5m2, 14)}[fmt]
    v = np.moveaxis(np.asarray(x, np.float32).astype(ml_dtypes.bfloat16).astype(np.float64), axis, -1)
    blocks = v.reshape(v.shape[:-1] + (-1, 32))
    amax = np.abs(blocks).max(-1, keepdims=True)
    byte = np.maximum(np.where(amax > 0, np.frexp(amax)[1] - 1 + 127, 0) - down, 1)
    scale = np.exp2(byte - 127.0)
    codes = (blocks / scale).astype(np.float32).astype(dtype).astype(np.float64)
    return np.moveaxis((codes * scale).reshape(v.shape), -1, axis)


WIDE = False


def mx_kscale(k):
    if not WIDE:
        return np.ones(k)
    levels = np.array([10, -10, 5, -5, 0])
    if k % 512:
        return np.exp2(np.random.permutation(np.resize(levels, k // 32))).repeat(32)
    a = np.empty((k // 512, 16))
    for p in range(k // 512):
        a[p, :8] = np.random.permutation(np.resize(levels, 8))
        for g in range(8):
            far = levels[np.abs(levels - a[p, g]) >= 10]
            a[p, g + 8] = far[np.random.randint(len(far))]
    return np.exp2(a.ravel()).repeat(32)


def f64(x):
    return np.asarray(x).astype(np.float64)


def striped(idx):
    return np.tile(np.asarray(idx).reshape(-1, 16).T, (8, 1)).astype(np.uint16)


def unstriped(offs):
    return offs[:16].T.reshape(-1).astype(np.int64)


E2M1 = np.array([0.0, 0.5, 1.0, 1.5, 2.0, 3.0, 4.0, 6.0, -0.0, -0.5, -1.0, -1.5, -2.0, -3.0, -4.0, -6.0])


def pack_weight(w, fmt):
    k, n = w.shape
    w = f64(np.asarray(w, np.float32).astype(ml_dtypes.bfloat16)).reshape(k // 32, 32, n)
    amax = np.abs(w).max(1)
    if fmt == "e4m3":
        byte = np.frexp(amax)[1] - 1 + 127 - 7
    else:
        mant, ex = np.frexp(amax / 6.0)
        byte = np.where(mant > 0.5, ex, ex - 1) + 127
    byte = np.clip(np.where(amax > 0, byte, 1), 1, 254)
    scaled = (w * np.exp2(127.0 - byte)[:, None, :]).reshape(k, n).astype(np.float32)
    by_word = np.ascontiguousarray(scaled.reshape(k // 512, 128, 4, n).transpose(0, 1, 3, 2))
    if fmt == "e4m3":
        words = by_word.astype(ml_dtypes.float8_e4m3fn).view(np.uint8)
    else:
        c = by_word.astype(ml_dtypes.float4_e2m1fn).view(np.uint8) & 0xF
        words = (c[..., 0::2] | (c[..., 1::2] << 4)).reshape(k // 512, 128, 2 * n)
    return np.ascontiguousarray(words), np.ascontiguousarray(byte.astype(np.uint8).reshape(k // 512, 16, n))


def unpack_weight(words, scales, fmt):
    g, _, n = scales.shape
    words = np.ascontiguousarray(words).reshape(g, 128, n, -1)
    if fmt == "e4m3":
        vals = words.view(ml_dtypes.float8_e4m3fn).astype(np.float64)
    else:
        nib = np.empty((g, 128, n, 4), np.uint8)
        nib[..., 0::2] = words & 0xF
        nib[..., 1::2] = words >> 4
        vals = E2M1[nib]
    vals = vals * np.repeat(np.exp2(scales.astype(np.float64) - 127.0), 8, axis=1)[..., None]
    return vals.transpose(0, 1, 3, 2).reshape(g * 512, n)


def bf(x):
    return np.asarray(x, np.float32).astype(ml_dtypes.bfloat16)


def planes(Y):
    r, m = Y.shape
    b = f64(bf(Y)).reshape(r // 32, 32, m)
    amax = np.abs(b).max(1)
    byte = np.clip(np.where(amax > 0, np.frexp(amax)[1] - 1 + 127 - 7, 1), 1, 254)
    codes = (b * np.exp2(127.0 - byte)[:, None, :]).reshape(r, m).astype(np.float32).astype(ml_dtypes.float8_e4m3fn).view(np.uint8)
    words = codes.reshape(r // 512, 128, 4, m).transpose(0, 1, 3, 2)
    return np.ascontiguousarray(words), np.ascontiguousarray(byte.astype(np.uint8).reshape(r // 512, 16, m))


K, T, V, J, L, N = 512, 1024, 512, 512, 512, 512


def setup_inputs():
    n = np.random.standard_normal
    idx = np.random.permutation(T)[:J]
    idx2 = np.random.randint(0, V, J)
    fk = mx_kscale(K)
    fl = mx_kscale(L)
    wap = pack_weight(n((K, N)) * 1 / np.sqrt(K) * fk[:, None], "e4m3")
    xsp = pack_weight(n((L, T)) / fl[:, None], "e2m1")
    wsp = pack_weight(n((L, N)) * 1 / np.sqrt(L) * fl[:, None], "e4m3")
    return {
        "xf": (n((K, T))).astype(np.float32),
        "cx": (n((K, V))).astype(np.float32),
        "fk": (np.random.uniform(0.5, 2.0, (K, 1)) / fk[:, None]).astype(np.float32),
        "wa_words": wap[0],
        "wa_scales": wap[1],
        "xs_words": xsp[0],
        "xs_scales": xsp[1],
        "ws_words": wsp[0],
        "ws_scales": wsp[1],
        "offs": striped(idx),
        "offs2": striped(idx2),
    }


def reference(xf, cx, fk, wa_words, wa_scales, xs_words, xs_scales, ws_words, ws_scales, offs, offs2):
    idx = unstriped(offs)
    idx2 = unstriped(offs2)
    wau = unpack_weight(wa_words, wa_scales, "e4m3")
    xsu = unpack_weight(xs_words, xs_scales, "e2m1")
    wsu = unpack_weight(ws_words, ws_scales, "e4m3")
    u = (f64(xf)[:, idx] + f64(cx)[:, idx2]) * f64(fk)
    uq = mxq(u, 0, "e4m3")
    p = wau.T @ uq
    d = np.maximum(p, 0.0)
    dp = np.zeros((N, T))
    dp[:, idx] = d
    z = wsu.T @ xsu
    y = z + dp
    words, scales = planes(y)
    return y, words, scales

@@ -1,0 +1,209 @@
+from contextlib import ExitStack
+
+import concourse.mybir as mybir
+
+K, T, V, J, L, N = 512, 1024, 512, 512, 512, 512
+FLOPS = 2 * K * N * J + 2 * L * N * T
+
+F32 = mybir.dt.float32
+BF16 = mybir.dt.bfloat16
+I32 = mybir.dt.int32
+U16 = mybir.dt.uint16
+U8 = mybir.dt.uint8
+FP8X4 = mybir.dt.float8_e4m3fn_x4
+FP4X4 = mybir.dt.float4_e2m1fn_x4
+ADD = mybir.AluOpType.add
+COPY = mybir.ActivationFunctionType.Copy
+RELU = mybir.ActivationFunctionType.Relu
+
+P = 128
+PACK = 4
+HALF = J // 2
+BANK = 512
+WA_ROW = 4
+
+
+def tile_moe_expert_reads_token_and_context_pl_kernel(
+    tc, xf, cx, fk, wa_words, wa_scales, xs_words, xs_scales, ws_words, ws_scales, offs, offs2, out_0, out_1, out_2
+):
+    nc = tc.nc
+    with ExitStack() as ctx:
+        sb = ctx.enter_context(tc.tile_pool(name="sb", bufs=1))
+        ps_p = ctx.enter_context(tc.psum_pool(name="ps_p", bufs=1))
+        ps_z = ctx.enter_context(tc.psum_pool(name="ps_z", bufs=4))
+
+        def tile(shape, dtype, name):
+            return sb.tile(shape, dtype, name=name, align_bytes=64)
+
+        tok_list = sb.tile([P, J // 16], U16, name="tok_list")
+        ctx_list = sb.tile([P, J // 16], U16, name="ctx_list")
+        x_sb = [tile([P, T], F32, f"x{j}") for j in range(PACK)]
+        c_sb = [tile([P, V], F32, f"c{j}") for j in range(PACK)]
+        fk_sb = tile([P, PACK], F32, "fk_sb")
+        wa_raw = tile([P, N], I32, "wa_raw")
+        ws_raw = tile([P, N], I32, "ws_raw")
+        wsc_raw = tile([P, N], U8, "wsc_raw")
+        wa_dealt = tile([P, N], I32, "wa_dealt")
+        ws_dealt = tile([P, N], I32, "ws_dealt")
+        wsc_dealt = tile([P, N], U8, "wsc_dealt")
+        xs_sb = tile([P, 2 * T], U8, "xs_sb")
+        xs_sc = tile([P, T], U8, "xs_sc")
+        dp = [tile([P, T], F32, f"dp{t}") for t in range(PACK)]
+
+        nc.vector.memset(wsc_raw[:].bitcast(I32), 0)
+        nc.vector.memset(xs_sc[:].bitcast(I32), 0)
+        for t in range(PACK - 1):
+            nc.vector.memset(dp[t][:], 0.0)
+        nc.gpsimd.memset(dp[PACK - 1][:], 0.0)
+
+        x_rows = xf.rearrange("(p j) t -> j p t", j=PACK)
+        c_rows = cx.rearrange("(p j) v -> j p v", j=PACK)
+
+        def load_scale_rows(plane, first, scales, r):
+            rows = scales[0].bitcast(I32).rearrange("(q r) c -> r q c", r=4)
+            nc.sync.dma_start(plane[:].bitcast(I32)[first + r : P : 32, :], rows[r])
+
+        nc.sync.dma_start(ctx_list[:], offs2)
+        nc.sync.dma_start(c_sb[0][:], c_rows[0])
+        nc.sync.dma_start(tok_list[:], offs)
+        nc.sync.dma_start(x_sb[0][:], x_rows[0])
+        nc.sync.dma_start(fk_sb[:], fk.rearrange("(p j) o -> p (j o)", j=PACK))
+        nc.sync.dma_start(c_sb[1][:], c_rows[1])
+        nc.sync.dma_start(x_sb[1][:], x_rows[1])
+        for i, (dst, src) in enumerate(((c_sb[2], c_rows[2]), (c_sb[3], c_rows[3]), (x_sb[2], x_rows[2]), (x_sb[3], x_rows[3]))):
+            load_scale_rows(wsc_raw, WA_ROW, wa_scales, i)
+            load_scale_rows(wsc_raw, 0, ws_scales, i)
+            nc.sync.dma_start(dst[:], src)
+        nc.sync.dma_start(wa_raw[:], wa_words[0].rearrange("p n r -> p (n r)").bitcast(I32))
+        nc.sync.dma_start(ws_raw[:], ws_words[0].rearrange("p n r -> p (n r)").bitcast(I32))
+        nc.sync.dma_start(xs_sb[:].bitcast(I32), xs_words[0].bitcast(I32))
+        for r in range(4):
+            load_scale_rows(xs_sc, 0, xs_scales, r)
+
+        def deal(dst, src, run):
+            nc.vector.tensor_copy(
+                dst[:].rearrange("p (t c i) -> p c t i", t=PACK, i=run),
+                src[:].rearrange("p (c i t) -> p c t i", t=PACK, i=run),
+            )
+
+        def entries(lst, h):
+            return lst[:, h * HALF // 16 : (h + 1) * HALF // 16]
+
+        picked = {(j, h): tile([P, HALF], F32, f"picked{j}{h}") for j in range(PACK) for h in range(2) if (j, h) != (2, 1)}
+        picked[(2, 1)] = picked[(3, 0)]
+        summed = {(j, h): tile([P, HALF], F32, f"summed{j}{h}") for j in range(PACK) for h in range(2)}
+        u_bf = [tile([P, HALF, PACK], BF16, f"u_bf{h}") for h in range(2)]
+        u_codes = [tile([P, HALF], I32, f"u_codes{h}") for h in range(2)]
+        u_sc = [tile([P, HALF], U8, f"u_sc{h}") for h in range(2)]
+        p_ps = [ps_p.tile([P, J], F32, name=f"p_ps{t}") for t in range(PACK)]
+        d_sb = [tile([P, J], F32, f"d{t}") for t in range(PACK)]
+
+        def pick_context(j, h):
+            nc.vector.tensor_copy(picked[(j, h)][:], c_sb[j][:].indirect(entries(ctx_list, h)))
+
+        def add_token(j, h):
+            nc.vector.tensor_tensor(summed[(j, h)][:], x_sb[j][:].indirect(entries(tok_list, h)), picked[(j, h)][:], ADD)
+            nc.scalar.activation(u_bf[h][:, :, j], summed[(j, h)][:], COPY, scale=fk_sb[:, j : j + 1])
+
+        def expert(h):
+            cols = slice(h * HALF, (h + 1) * HALF)
+            nc.vector.quantize_mx(out=u_codes[h][:].bitcast(FP8X4), scales=u_sc[h][:], in_=u_bf[h][:].rearrange("p c j -> p (c j)"))
+            for t in range(PACK):
+                m = slice(t * P, (t + 1) * P)
+                nc.tensor.matmul_mx(
+                    out=p_ps[t][:, cols],
+                    lhsT=wa_dealt[:, m].bitcast(FP8X4),
+                    lhsT_scale=wsc_dealt[WA_ROW:P, m],
+                    rhs=u_codes[h][:].bitcast(FP8X4),
+                    rhs_scale=u_sc[h][:],
+                    start=True,
+                    stop=True,
+                )
+                nc.scalar.activation(d_sb[t][:, cols], p_ps[t][:, cols], RELU)
+
+        def scatter(t, h):
+            cols = slice(h * HALF, (h + 1) * HALF)
+            nc.vector.tensor_copy(dp[t][:].indirect(entries(tok_list, h)), d_sb[t][:, cols])
+
+        for j in (0, 1):
+            pick_context(j, 0)
+            pick_context(j, 1)
+            add_token(j, 0)
+            add_token(j, 1)
+        pick_context(2, 0)
+        pick_context(3, 0)
+        add_token(2, 0)
+        pick_context(3, 1)
+        deal(wsc_dealt, wsc_raw, 16)
+        add_token(3, 0)
+        add_token(3, 1)
+        pick_context(2, 1)
+        deal(wa_dealt, wa_raw, 4)
+        expert(0)
+        add_token(2, 1)
+        deal(ws_dealt, ws_raw, 4)
+        scatter(0, 0)
+        expert(1)
+        scatter(1, 0)
+        scatter(0, 1)
+        scatter(1, 1)
+        for t in (2, 3):
+            nc.vector.tensor_copy(dp[t][:].indirect(tok_list[:]), d_sb[t][:])
+
+        y_pair = [tile([P, 2, T], F32, f"y_pair{a}") for a in range(2)]
+        z_sb = [tile([P, T], F32, f"z{t}") for t in range(PACK - 1)]
+        y_bf = tile([P, T, PACK], BF16, "y_bf")
+        y_codes = tile([P, T], I32, "y_codes")
+        y_sc = tile([P, T], U8, "y_sc")
+        y_rows = out_0.rearrange("(p t) c -> t p c", t=PACK)
+        words_out = out_1[0].rearrange("p c r -> p (c r)").bitcast(I32)
+
+        def shared(t, g):
+            m = slice(t * P, (t + 1) * P)
+            z_ps = ps_z.tile([P, BANK], F32, name="z_ps")
+            nc.tensor.matmul_mx(
+                out=z_ps[:],
+                lhsT=ws_dealt[:, m].bitcast(FP8X4),
+                lhsT_scale=wsc_dealt[:, m],
+                rhs=xs_sb[:, 2 * g * BANK : 2 * (g + 1) * BANK].bitcast(FP4X4),
+                rhs_scale=xs_sc[:, g * BANK : (g + 1) * BANK],
+                start=True,
+                stop=True,
+            )
+            return z_ps
+
+        def rounded(a, lo, hi):
+            return y_bf[:, lo:hi, 2 * a : 2 * a + 2], y_pair[a][:, :, lo:hi].rearrange("p t c -> p c t")
+
+        for t in range(PACK - 1):
+            for g in range(2):
+                nc.scalar.copy(z_sb[t][:, g * BANK : (g + 1) * BANK], shared(t, g)[:])
+            y_t = y_pair[t // 2][:, t % 2, :]
+            nc.gpsimd.tensor_tensor(y_t, z_sb[t][:], dp[t][:], ADD)
+            nc.sync.dma_start(y_rows[t], y_t)
+            if t == 1:
+                nc.scalar.copy(*rounded(0, 0, T))
+
+        last = PACK - 1
+        for g in range(2):
+            z_ps = shared(last, g)
+            for q in range(2):
+                lo = g * BANK + q * 256
+                nc.vector.tensor_tensor(y_pair[1][:, 1, lo : lo + 256], z_ps[:, q * 256 : (q + 1) * 256], dp[last][:, lo : lo + 256], ADD)
+            nc.sync.dma_start(y_rows[last][:, g * BANK : (g + 1) * BANK], y_pair[1][:, 1, g * BANK : (g + 1) * BANK])
+        for lo, hi in ((0, 256), (256, 512), (512, 640)):
+            nc.scalar.copy(*rounded(1, lo, hi))
+        nc.vector.tensor_copy(*rounded(1, 640, T))
+        for lo in (0, 256, 768, 512):
+            nc.vector.quantize_mx(
+                out=y_codes[:, lo : lo + 256].bitcast(FP8X4),
+                scales=y_sc[:, lo : lo + 256],
+                in_=y_bf[:, lo : lo + 256, :].rearrange("p c t -> p (c t)"),
+            )
+            if lo == 256:
+                nc.sync.dma_start(words_out[:, 0:512], y_codes[:, 0:512])
+        nc.sync.dma_start(words_out[:, 512:T], y_codes[:, 512:T])
+        sc_rows = out_2[0].bitcast(I32).rearrange("(q r) c -> r q c", r=4)
+        for r in range(4):
+            eng = nc.scalar if r % 2 else nc.sync
+            eng.dma_start(sc_rows[r], y_sc[:].bitcast(I32)[r:P:32, :])

@@ -21,6 +21,7 @@ PACK = 4
 HALF = J // 2
 BANK = 512
 WA_ROW = 4
+WIDE = 704
 
 
 def tile_moe_expert_reads_token_and_context_pl_kernel(
@@ -38,7 +39,7 @@ def tile_moe_expert_reads_token_and_context_pl_kernel(
         tok_list = sb.tile([P, J // 16], U16, name="tok_list")
         ctx_list = sb.tile([P, J // 16], U16, name="ctx_list")
         x_sb = [tile([P, T], F32, f"x{j}") for j in range(PACK)]
-        c_sb = [tile([P, V], F32, f"c{j}") for j in range(PACK)]
+        c_sb = [tile([P, V if j == 2 else WIDE], F32, f"c{j}") for j in range(PACK)]
         fk_sb = tile([P, PACK], F32, "fk_sb")
         wa_raw = tile([P, N], I32, "wa_raw")
         ws_raw = tile([P, N], I32, "ws_raw")
@@ -50,11 +51,12 @@ def tile_moe_expert_reads_token_and_context_pl_kernel(
         xs_sc = tile([P, T], U8, "xs_sc")
         dp = [tile([P, T], F32, f"dp{t}") for t in range(PACK)]
 
-        nc.vector.memset(wsc_raw[:].bitcast(I32), 0)
-        nc.vector.memset(xs_sc[:].bitcast(I32), 0)
-        for t in range(PACK - 1):
-            nc.vector.memset(dp[t][:], 0.0)
-        nc.gpsimd.memset(dp[PACK - 1][:], 0.0)
+        nc.gpsimd.memset(wsc_raw[:].bitcast(I32), 0)
+        for j in (0, 1, 3):
+            nc.gpsimd.memset(c_sb[j][:, V:WIDE], 0.0)
+        nc.gpsimd.memset(xs_sc[:].bitcast(I32), 0)
+        for t in range(PACK):
+            nc.gpsimd.memset(dp[t][:], 0.0)
 
         x_rows = xf.rearrange("(p j) t -> j p t", j=PACK)
         c_rows = cx.rearrange("(p j) v -> j p v", j=PACK)
@@ -63,17 +65,17 @@ def tile_moe_expert_reads_token_and_context_pl_kernel(
             rows = scales[0].bitcast(I32).rearrange("(q r) c -> r q c", r=4)
             nc.sync.dma_start(plane[:].bitcast(I32)[first + r : P : 32, :], rows[r])
 
+        nc.scalar.dma_start(fk_sb[:], fk.rearrange("(p j) o -> p (j o)", j=PACK))
+        nc.sync.dma_start(c_sb[0][:, 0:V], c_rows[0])
         nc.sync.dma_start(ctx_list[:], offs2)
-        nc.sync.dma_start(c_sb[0][:], c_rows[0])
+        nc.sync.dma_start(c_sb[1][:, 0:V], c_rows[1])
         nc.sync.dma_start(tok_list[:], offs)
         nc.sync.dma_start(x_sb[0][:], x_rows[0])
-        nc.sync.dma_start(fk_sb[:], fk.rearrange("(p j) o -> p (j o)", j=PACK))
-        nc.sync.dma_start(c_sb[1][:], c_rows[1])
         nc.sync.dma_start(x_sb[1][:], x_rows[1])
-        for i, (dst, src) in enumerate(((c_sb[2], c_rows[2]), (c_sb[3], c_rows[3]), (x_sb[2], x_rows[2]), (x_sb[3], x_rows[3]))):
+        for i, (dst, src) in enumerate(((c_sb[2][:], c_rows[2]), (c_sb[3][:, 0:V], c_rows[3]), (x_sb[2][:], x_rows[2]), (x_sb[3][:], x_rows[3]))):
             load_scale_rows(wsc_raw, WA_ROW, wa_scales, i)
             load_scale_rows(wsc_raw, 0, ws_scales, i)
-            nc.sync.dma_start(dst[:], src)
+            nc.sync.dma_start(dst, src)
         nc.sync.dma_start(wa_raw[:], wa_words[0].rearrange("p n r -> p (n r)").bitcast(I32))
         nc.sync.dma_start(ws_raw[:], ws_words[0].rearrange("p n r -> p (n r)").bitcast(I32))
         nc.sync.dma_start(xs_sb[:].bitcast(I32), xs_words[0].bitcast(I32))
@@ -89,25 +91,31 @@ def tile_moe_expert_reads_token_and_context_pl_kernel(
         def entries(lst, h):
             return lst[:, h * HALF // 16 : (h + 1) * HALF // 16]
 
-        picked = {(j, h): tile([P, HALF], F32, f"picked{j}{h}") for j in range(PACK) for h in range(2) if (j, h) != (2, 1)}
-        picked[(2, 1)] = picked[(3, 0)]
-        summed = {(j, h): tile([P, HALF], F32, f"summed{j}{h}") for j in range(PACK) for h in range(2)}
-        u_bf = [tile([P, HALF, PACK], BF16, f"u_bf{h}") for h in range(2)]
+        summed = {(j, h): tile([P, HALF], F32, f"summed{j}{h}")[:] for j, h in ((2, 0), (3, 0), (3, 1))}
+        picked_all = {j: tile([P, J], F32, f"picked_all{j}") for j in (0, 1, 3)}
+        picked_2 = tile([P, HALF], F32, "picked_2")
+        picked = {(2, 0): picked_2[:], (2, 1): picked_all[3][:, 0:HALF], (3, 0): picked_all[3][:, 0:HALF], (3, 1): picked_all[3][:, HALF:J]}
+        summed_all = [tile([P, J], F32, f"summed_all{j}") for j in range(2)]
+        u_bf = tile([P, J, PACK], BF16, "u_bf")
+        summed[(2, 1)] = u_bf[:].rearrange("p c j -> p (c j)").bitcast(F32)[:, 0:HALF]
         u_codes = [tile([P, HALF], I32, f"u_codes{h}") for h in range(2)]
         u_sc = [tile([P, HALF], U8, f"u_sc{h}") for h in range(2)]
         p_ps = [ps_p.tile([P, J], F32, name=f"p_ps{t}") for t in range(PACK)]
         d_sb = [tile([P, J], F32, f"d{t}") for t in range(PACK)]
 
+        d_half = {(t, h): d_sb[t][:, h * HALF : (h + 1) * HALF] for t in range(2) for h in range(2)}
+        d_half[(1, 0)] = summed[(2, 1)]
+
         def pick_context(j, h):
-            nc.vector.tensor_copy(picked[(j, h)][:], c_sb[j][:].indirect(entries(ctx_list, h)))
+            nc.vector.tensor_copy(picked[(j, h)], c_sb[j][:].indirect(entries(ctx_list, h)))
 
         def add_token(j, h):
-            nc.vector.tensor_tensor(summed[(j, h)][:], x_sb[j][:].indirect(entries(tok_list, h)), picked[(j, h)][:], ADD)
-            nc.scalar.activation(u_bf[h][:, :, j], summed[(j, h)][:], COPY, scale=fk_sb[:, j : j + 1])
+            nc.vector.tensor_tensor(summed[(j, h)], x_sb[j][:].indirect(entries(tok_list, h)), picked[(j, h)], ADD)
+            nc.scalar.activation(u_bf[:, h * HALF : (h + 1) * HALF, j], summed[(j, h)], COPY, scale=fk_sb[:, j : j + 1])
 
         def expert(h):
             cols = slice(h * HALF, (h + 1) * HALF)
-            nc.vector.quantize_mx(out=u_codes[h][:].bitcast(FP8X4), scales=u_sc[h][:], in_=u_bf[h][:].rearrange("p c j -> p (c j)"))
+            nc.vector.quantize_mx(out=u_codes[h][:].bitcast(FP8X4), scales=u_sc[h][:], in_=u_bf[:, cols, :].rearrange("p c j -> p (c j)"))
             for t in range(PACK):
                 m = slice(t * P, (t + 1) * P)
                 nc.tensor.matmul_mx(
@@ -119,31 +127,38 @@ def tile_moe_expert_reads_token_and_context_pl_kernel(
                     start=True,
                     stop=True,
                 )
-                nc.scalar.activation(d_sb[t][:, cols], p_ps[t][:, cols], RELU)
+
+        def relu(t, h):
+            cols = slice(h * HALF, (h + 1) * HALF)
+            nc.scalar.activation(d_half[(t, h)], p_ps[t][:, cols], RELU)
 
         def scatter(t, h):
-            cols = slice(h * HALF, (h + 1) * HALF)
-            nc.vector.tensor_copy(dp[t][:].indirect(entries(tok_list, h)), d_sb[t][:, cols])
+            nc.vector.tensor_copy(dp[t][:].indirect(entries(tok_list, h)), d_half[(t, h)])
 
         for j in (0, 1):
-            pick_context(j, 0)
-            pick_context(j, 1)
-            add_token(j, 0)
-            add_token(j, 1)
+            nc.vector.tensor_copy(picked_all[j][:], c_sb[j][:].indirect(ctx_list[:]))
+        for j in (0, 1):
+            nc.vector.tensor_tensor(summed_all[j][:], x_sb[j][:].indirect(tok_list[:]), picked_all[j][:], ADD)
+            nc.scalar.activation(u_bf[:, :, j], summed_all[j][:], COPY, scale=fk_sb[:, j : j + 1])
         pick_context(2, 0)
-        pick_context(3, 0)
+        nc.vector.tensor_copy(picked_all[3][:], c_sb[3][:].indirect(ctx_list[:]))
         add_token(2, 0)
-        pick_context(3, 1)
         deal(wsc_dealt, wsc_raw, 16)
         add_token(3, 0)
         add_token(3, 1)
         pick_context(2, 1)
         deal(wa_dealt, wa_raw, 4)
         expert(0)
-        add_token(2, 1)
+        relu(0, 0)
         deal(ws_dealt, ws_raw, 4)
+        add_token(2, 1)
         scatter(0, 0)
+        relu(1, 0)
         expert(1)
+        relu(0, 1)
+        relu(1, 1)
+        for t in (2, 3):
+            nc.scalar.activation(d_sb[t][:], p_ps[t][:], RELU)
         scatter(1, 0)
         scatter(0, 1)
         scatter(1, 1)
@@ -152,6 +167,7 @@ def tile_moe_expert_reads_token_and_context_pl_kernel(
 
         y_pair = [tile([P, 2, T], F32, f"y_pair{a}") for a in range(2)]
         z_sb = [tile([P, T], F32, f"z{t}") for t in range(PACK - 1)]
+        z_end = tile([P, 256], F32, "z_end")
         y_bf = tile([P, T, PACK], BF16, "y_bf")
         y_codes = tile([P, T], I32, "y_codes")
         y_sc = tile([P, T], U8, "y_sc")
@@ -176,33 +192,38 @@ def tile_moe_expert_reads_token_and_context_pl_kernel(
             return y_bf[:, lo:hi, 2 * a : 2 * a + 2], y_pair[a][:, :, lo:hi].rearrange("p t c -> p c t")
 
         for t in range(PACK - 1):
-            for g in range(2):
-                nc.scalar.copy(z_sb[t][:, g * BANK : (g + 1) * BANK], shared(t, g)[:])
             y_t = y_pair[t // 2][:, t % 2, :]
-            nc.gpsimd.tensor_tensor(y_t, z_sb[t][:], dp[t][:], ADD)
+            for g in range(2):
+                cols = slice(g * BANK, (g + 1) * BANK)
+                nc.scalar.copy(z_sb[t][:, cols], shared(t, g)[:])
+                nc.gpsimd.tensor_tensor(y_t[:, cols], z_sb[t][:, cols], dp[t][:, cols], ADD)
             nc.sync.dma_start(y_rows[t], y_t)
-            if t == 1:
-                nc.scalar.copy(*rounded(0, 0, T))
 
         last = PACK - 1
+        z_last = [shared(last, g) for g in range(2)]
+        nc.scalar.copy(z_end[:], z_last[1][:, 256:BANK])
         for g in range(2):
-            z_ps = shared(last, g)
-            for q in range(2):
-                lo = g * BANK + q * 256
-                nc.vector.tensor_tensor(y_pair[1][:, 1, lo : lo + 256], z_ps[:, q * 256 : (q + 1) * 256], dp[last][:, lo : lo + 256], ADD)
-            nc.sync.dma_start(y_rows[last][:, g * BANK : (g + 1) * BANK], y_pair[1][:, 1, g * BANK : (g + 1) * BANK])
-        for lo, hi in ((0, 256), (256, 512), (512, 640)):
+            nc.scalar.copy(*rounded(0, g * BANK, (g + 1) * BANK))
+        y_last = y_pair[1][:, 1, :]
+        for lo, hi in ((0, 128), (128, 512), (512, 768)):
+            g = lo // BANK
+            nc.vector.tensor_tensor(y_last[:, lo:hi], z_last[g][:, lo - g * BANK : hi - g * BANK], dp[last][:, lo:hi], ADD)
+        nc.gpsimd.tensor_tensor(y_last[:, 768:T], z_end[:], dp[last][:, 768:T], ADD)
+        for g in range(2):
+            nc.sync.dma_start(y_rows[last][:, g * BANK : (g + 1) * BANK], y_last[:, g * BANK : (g + 1) * BANK])
+        for lo, hi in ((0, 128), (128, 256), (256, 512)):
             nc.scalar.copy(*rounded(1, lo, hi))
-        nc.vector.tensor_copy(*rounded(1, 640, T))
-        for lo in (0, 256, 768, 512):
+        nc.vector.tensor_copy(
+            y_bf[:, 512:T, 2:4].rearrange("p (c i) t -> p c t i", i=4),
+            y_pair[1][:, :, 512:T].rearrange("p t (c i) -> p c t i", i=4),
+        )
+        for lo, hi in ((0, 256), (512, T), (256, 512)):
             nc.vector.quantize_mx(
-                out=y_codes[:, lo : lo + 256].bitcast(FP8X4),
-                scales=y_sc[:, lo : lo + 256],
-                in_=y_bf[:, lo : lo + 256, :].rearrange("p c t -> p (c t)"),
+                out=y_codes[:, lo:hi].bitcast(FP8X4),
+                scales=y_sc[:, lo:hi],
+                in_=y_bf[:, lo:hi, :].rearrange("p c t -> p (c t)"),
             )
-            if lo == 256:
-                nc.sync.dma_start(words_out[:, 0:512], y_codes[:, 0:512])
-        nc.sync.dma_start(words_out[:, 512:T], y_codes[:, 512:T])
+            nc.sync.dma_start(words_out[:, lo:hi], y_codes[:, lo:hi])
         sc_rows = out_2[0].bitcast(I32).rearrange("(q r) c -> r q c", r=4)
         for r in range(4):
             eng = nc.scalar if r % 2 else nc.sync

@@ -38,49 +38,52 @@ def tile_moe_expert_reads_token_and_context_pl_kernel(
 
         tok_list = sb.tile([P, J // 16], U16, name="tok_list")
         ctx_list = sb.tile([P, J // 16], U16, name="ctx_list")
-        x_sb = [tile([P, T], F32, f"x{j}") for j in range(PACK)]
-        c_sb = [tile([P, V if j == 2 else WIDE], F32, f"c{j}") for j in range(PACK)]
+        x_sb = [sb.tile([P, T], F32, name=f"x{j}", tag=f"x{j}", align_bytes=64) for j in range(PACK)]
+        c_sb = tile([P, 3 * V + WIDE], F32, "c_sb")
+        c_at = (3 * V, 2 * V, 0, V)
         fk_sb = tile([P, PACK], F32, "fk_sb")
-        wa_raw = tile([P, N], I32, "wa_raw")
+        wa_raw = sb.tile([P, N], I32, name="wa_raw", tag="wa_raw", align_bytes=64)
         ws_raw = tile([P, N], I32, "ws_raw")
-        wsc_raw = tile([P, N], U8, "wsc_raw")
+        wsc_raw = sb.tile([P, N], U8, name="wsc_raw", tag="wsc_raw", align_bytes=64)
         wa_dealt = tile([P, N], I32, "wa_dealt")
         ws_dealt = tile([P, N], I32, "ws_dealt")
         wsc_dealt = tile([P, N], U8, "wsc_dealt")
         xs_sb = tile([P, 2 * T], U8, "xs_sb")
         xs_sc = tile([P, T], U8, "xs_sc")
-        dp = [tile([P, T], F32, f"dp{t}") for t in range(PACK)]
+        dp = [tile([P, T], F32, f"dp{t}") for t in range(2)]
 
         nc.gpsimd.memset(wsc_raw[:].bitcast(I32), 0)
-        for j in (0, 1, 3):
-            nc.gpsimd.memset(c_sb[j][:, V:WIDE], 0.0)
-        nc.gpsimd.memset(xs_sc[:].bitcast(I32), 0)
-        for t in range(PACK):
+        nc.vector.memset(c_sb[:, 4 * V : 3 * V + WIDE], 0.0)
+        nc.vector.memset(xs_sc[:].bitcast(I32), 0)
+        for t in range(2):
             nc.gpsimd.memset(dp[t][:], 0.0)
 
         x_rows = xf.rearrange("(p j) t -> j p t", j=PACK)
         c_rows = cx.rearrange("(p j) v -> j p v", j=PACK)
 
-        def load_scale_rows(plane, first, scales, r):
-            rows = scales[0].bitcast(I32).rearrange("(q r) c -> r q c", r=4)
-            nc.sync.dma_start(plane[:].bitcast(I32)[first + r : P : 32, :], rows[r])
+        def load_scale_rows(eng, plane, first, scales, r):
+            eng.dma_start(plane[:].bitcast(I32)[32 * r + first : 32 * r + first + 4, :], scales[0].bitcast(I32)[4 * r : 4 * r + 4, :])
 
         nc.scalar.dma_start(fk_sb[:], fk.rearrange("(p j) o -> p (j o)", j=PACK))
-        nc.sync.dma_start(c_sb[0][:, 0:V], c_rows[0])
+        nc.sync.dma_start(c_sb[:, c_at[0] : c_at[0] + V], c_rows[0])
         nc.sync.dma_start(ctx_list[:], offs2)
-        nc.sync.dma_start(c_sb[1][:, 0:V], c_rows[1])
+        nc.sync.dma_start(c_sb[:, c_at[1] : c_at[1] + V], c_rows[1])
         nc.sync.dma_start(tok_list[:], offs)
         nc.sync.dma_start(x_sb[0][:], x_rows[0])
         nc.sync.dma_start(x_sb[1][:], x_rows[1])
-        for i, (dst, src) in enumerate(((c_sb[2][:], c_rows[2]), (c_sb[3][:, 0:V], c_rows[3]), (x_sb[2][:], x_rows[2]), (x_sb[3][:], x_rows[3]))):
-            load_scale_rows(wsc_raw, WA_ROW, wa_scales, i)
-            load_scale_rows(wsc_raw, 0, ws_scales, i)
-            nc.sync.dma_start(dst, src)
+        nc.sync.dma_start(c_sb[:, c_at[2] : c_at[2] + V], c_rows[2])
+        for r in range(4):
+            load_scale_rows(nc.sync, wsc_raw, 0, ws_scales, r)
+        nc.sync.dma_start(c_sb[:, c_at[3] : c_at[3] + V], c_rows[3])
+        nc.sync.dma_start(x_sb[2][:], x_rows[2])
+        nc.sync.dma_start(x_sb[3][:], x_rows[3])
+        for r in range(4):
+            load_scale_rows(nc.sync, wsc_raw, WA_ROW, wa_scales, r)
         nc.sync.dma_start(wa_raw[:], wa_words[0].rearrange("p n r -> p (n r)").bitcast(I32))
         nc.sync.dma_start(ws_raw[:], ws_words[0].rearrange("p n r -> p (n r)").bitcast(I32))
         nc.sync.dma_start(xs_sb[:].bitcast(I32), xs_words[0].bitcast(I32))
         for r in range(4):
-            load_scale_rows(xs_sc, 0, xs_scales, r)
+            load_scale_rows(nc.sync, xs_sc, 0, xs_scales, r)
 
         def deal(dst, src, run):
             nc.vector.tensor_copy(
@@ -96,10 +99,10 @@ def tile_moe_expert_reads_token_and_context_pl_kernel(
         picked_2 = tile([P, HALF], F32, "picked_2")
         picked = {(2, 0): picked_2[:], (2, 1): picked_all[3][:, 0:HALF], (3, 0): picked_all[3][:, 0:HALF], (3, 1): picked_all[3][:, HALF:J]}
         summed_all = [tile([P, J], F32, f"summed_all{j}") for j in range(2)]
-        u_bf = tile([P, J, PACK], BF16, "u_bf")
+        u_bf = sb.tile([P, J, PACK], BF16, name="u_bf", tag="u_bf", align_bytes=64)
         summed[(2, 1)] = u_bf[:].rearrange("p c j -> p (c j)").bitcast(F32)[:, 0:HALF]
-        u_codes = [tile([P, HALF], I32, f"u_codes{h}") for h in range(2)]
-        u_sc = [tile([P, HALF], U8, f"u_sc{h}") for h in range(2)]
+        u_codes = {1: tile([P, HALF], I32, "u_codes1")}
+        u_sc = {1: tile([P, HALF], U8, "u_sc1")}
         p_ps = [ps_p.tile([P, J], F32, name=f"p_ps{t}") for t in range(PACK)]
         d_sb = [tile([P, J], F32, f"d{t}") for t in range(PACK)]
 
@@ -107,7 +110,7 @@ def tile_moe_expert_reads_token_and_context_pl_kernel(
         d_half[(1, 0)] = summed[(2, 1)]
 
         def pick_context(j, h):
-            nc.vector.tensor_copy(picked[(j, h)], c_sb[j][:].indirect(entries(ctx_list, h)))
+            nc.vector.tensor_copy(picked[(j, h)], c_sb[:, 0:V].indirect(entries(ctx_list, h)))
 
         def add_token(j, h):
             nc.vector.tensor_tensor(summed[(j, h)], x_sb[j][:].indirect(entries(tok_list, h)), picked[(j, h)], ADD)
@@ -136,18 +139,20 @@ def tile_moe_expert_reads_token_and_context_pl_kernel(
             nc.vector.tensor_copy(dp[t][:].indirect(entries(tok_list, h)), d_half[(t, h)])
 
         for j in (0, 1):
-            nc.vector.tensor_copy(picked_all[j][:], c_sb[j][:].indirect(ctx_list[:]))
+            nc.vector.tensor_copy(picked_all[j][:], c_sb[:, c_at[j] : c_at[j] + WIDE].indirect(ctx_list[:]))
         for j in (0, 1):
             nc.vector.tensor_tensor(summed_all[j][:], x_sb[j][:].indirect(tok_list[:]), picked_all[j][:], ADD)
             nc.scalar.activation(u_bf[:, :, j], summed_all[j][:], COPY, scale=fk_sb[:, j : j + 1])
         pick_context(2, 0)
-        nc.vector.tensor_copy(picked_all[3][:], c_sb[3][:].indirect(ctx_list[:]))
+        nc.vector.tensor_copy(picked_all[3][:], c_sb[:, V : V + WIDE].indirect(ctx_list[:]))
         add_token(2, 0)
-        deal(wsc_dealt, wsc_raw, 16)
         add_token(3, 0)
         add_token(3, 1)
         pick_context(2, 1)
+        deal(wsc_dealt, wsc_raw, 16)
         deal(wa_dealt, wa_raw, 4)
+        u_codes[0] = sb.tile([P, HALF], I32, name="u_codes0", tag="wa_raw", align_bytes=64)
+        u_sc[0] = sb.tile([P, HALF], U8, name="u_sc0", tag="wsc_raw", align_bytes=64)
         expert(0)
         relu(0, 0)
         deal(ws_dealt, ws_raw, 4)
@@ -162,11 +167,13 @@ def tile_moe_expert_reads_token_and_context_pl_kernel(
         scatter(1, 0)
         scatter(0, 1)
         scatter(1, 1)
-        for t in (2, 3):
+        for t, tag in ((2, "x2"), (3, "u_bf")):
+            dp.append(sb.tile([P, T], F32, name=f"dp{t}", tag=tag, align_bytes=64))
+            nc.gpsimd.memset(dp[t][:], 0.0)
             nc.vector.tensor_copy(dp[t][:].indirect(tok_list[:]), d_sb[t][:])
 
         y_pair = [tile([P, 2, T], F32, f"y_pair{a}") for a in range(2)]
-        z_sb = [tile([P, T], F32, f"z{t}") for t in range(PACK - 1)]
+        z_sb = [tile([P, T], F32, f"z{t}")[:] for t in range(2)] + [y_pair[1][:, 1, :]]
         z_end = tile([P, 256], F32, "z_end")
         y_bf = tile([P, T, PACK], BF16, "y_bf")
         y_codes = tile([P, T], I32, "y_codes")
@@ -205,19 +212,19 @@ def tile_moe_expert_reads_token_and_context_pl_kernel(
         for g in range(2):
             nc.scalar.copy(*rounded(0, g * BANK, (g + 1) * BANK))
         y_last = y_pair[1][:, 1, :]
-        for lo, hi in ((0, 128), (128, 512), (512, 768)):
+        for lo, hi in ((0, 256), (512, 768), (256, 512)):
             g = lo // BANK
             nc.vector.tensor_tensor(y_last[:, lo:hi], z_last[g][:, lo - g * BANK : hi - g * BANK], dp[last][:, lo:hi], ADD)
         nc.gpsimd.tensor_tensor(y_last[:, 768:T], z_end[:], dp[last][:, 768:T], ADD)
         for g in range(2):
             nc.sync.dma_start(y_rows[last][:, g * BANK : (g + 1) * BANK], y_last[:, g * BANK : (g + 1) * BANK])
-        for lo, hi in ((0, 128), (128, 256), (256, 512)):
+        for lo, hi in ((0, 256), (256, 512)):
             nc.scalar.copy(*rounded(1, lo, hi))
         nc.vector.tensor_copy(
             y_bf[:, 512:T, 2:4].rearrange("p (c i) t -> p c t i", i=4),
             y_pair[1][:, :, 512:T].rearrange("p t (c i) -> p c t i", i=4),
         )
-        for lo, hi in ((0, 256), (512, T), (256, 512)):
+        for lo, hi in ((0, 256), (768, T), (512, 768), (256, 512)):
             nc.vector.quantize_mx(
                 out=y_codes[:, lo:hi].bitcast(FP8X4),
                 scales=y_sc[:, lo:hi],

@@ -18,10 +18,16 @@ RELU = mybir.ActivationFunctionType.Relu
 
 P = 128
 PACK = 4
+LIST_ROWS = 16
 HALF = J // 2
 BANK = 512
+Z_BANKS = 4
+QUADRANT = 32
 WA_ROW = 4
 WIDE = 704
+QUARTER = T // 4
+POOL_FROM = 3 * QUARTER
+VECTOR_FROM = 640
 
 
 def tile_moe_expert_reads_token_and_context_pl_kernel(
@@ -31,98 +37,113 @@ def tile_moe_expert_reads_token_and_context_pl_kernel(
     with ExitStack() as ctx:
         sb = ctx.enter_context(tc.tile_pool(name="sb", bufs=1))
         ps_p = ctx.enter_context(tc.psum_pool(name="ps_p", bufs=1))
-        ps_z = ctx.enter_context(tc.psum_pool(name="ps_z", bufs=4))
+        ps_z = ctx.enter_context(tc.psum_pool(name="ps_z", bufs=Z_BANKS))
 
-        def tile(shape, dtype, name):
-            return sb.tile(shape, dtype, name=name, align_bytes=64)
+        def tile(shape, dtype, name, tag=None):
+            return sb.tile(shape, dtype, name=name, tag=tag or name, align_bytes=64)
 
-        tok_list = sb.tile([P, J // 16], U16, name="tok_list")
-        ctx_list = sb.tile([P, J // 16], U16, name="ctx_list")
-        x_sb = [sb.tile([P, T], F32, name=f"x{j}", tag=f"x{j}", align_bytes=64) for j in range(PACK)]
+        tok_list = sb.tile([P, J // LIST_ROWS], U16, name="tok_list")
+        ctx_list = sb.tile([P, J // LIST_ROWS], U16, name="ctx_list")
+        x_sb = [tile([P, T], F32, f"x{r}") for r in range(PACK)]
         c_sb = tile([P, 3 * V + WIDE], F32, "c_sb")
         c_at = (3 * V, 2 * V, 0, V)
         fk_sb = tile([P, PACK], F32, "fk_sb")
-        wa_raw = sb.tile([P, N], I32, name="wa_raw", tag="wa_raw", align_bytes=64)
+        wa_raw = tile([P, N], I32, "wa_raw")
         ws_raw = tile([P, N], I32, "ws_raw")
-        wsc_raw = sb.tile([P, N], U8, name="wsc_raw", tag="wsc_raw", align_bytes=64)
+        wsc_raw = tile([P, N], U8, "wsc_raw")
         wa_dealt = tile([P, N], I32, "wa_dealt")
         ws_dealt = tile([P, N], I32, "ws_dealt")
         wsc_dealt = tile([P, N], U8, "wsc_dealt")
         xs_sb = tile([P, 2 * T], U8, "xs_sb")
         xs_sc = tile([P, T], U8, "xs_sc")
-        dp = [tile([P, T], F32, f"dp{t}") for t in range(2)]
+        dp = [tile([P, T], F32, f"dp{r}") for r in range(2)]
 
         nc.gpsimd.memset(wsc_raw[:].bitcast(I32), 0)
-        nc.vector.memset(c_sb[:, 4 * V : 3 * V + WIDE], 0.0)
+        nc.vector.memset(c_sb[:, PACK * V : 3 * V + WIDE], 0.0)
         nc.vector.memset(xs_sc[:].bitcast(I32), 0)
-        for t in range(2):
-            nc.gpsimd.memset(dp[t][:], 0.0)
+        for r in range(2):
+            nc.gpsimd.memset(dp[r][:], 0.0)
 
-        x_rows = xf.rearrange("(p j) t -> j p t", j=PACK)
-        c_rows = cx.rearrange("(p j) v -> j p v", j=PACK)
+        x_planes = xf.rearrange("(p r) t -> r p t", r=PACK)
+        c_planes = cx.rearrange("(p r) v -> r p v", r=PACK)
 
-        def load_scale_rows(eng, plane, first, scales, r):
-            eng.dma_start(plane[:].bitcast(I32)[32 * r + first : 32 * r + first + 4, :], scales[0].bitcast(I32)[4 * r : 4 * r + 4, :])
+        def load_contexts(r):
+            nc.sync.dma_start(c_sb[:, c_at[r] : c_at[r] + V], c_planes[r])
 
-        nc.scalar.dma_start(fk_sb[:], fk.rearrange("(p j) o -> p (j o)", j=PACK))
-        nc.sync.dma_start(c_sb[:, c_at[0] : c_at[0] + V], c_rows[0])
+        def load_scales(plane, first, scales):
+            for q in range(P // QUADRANT):
+                at = QUADRANT * q + first
+                nc.sync.dma_start(plane[:].bitcast(I32)[at : at + 4, :], scales[0].bitcast(I32)[4 * q : 4 * q + 4, :])
+
+        nc.scalar.dma_start(fk_sb[:], fk.rearrange("(p r) o -> p (r o)", r=PACK))
+        load_contexts(0)
         nc.sync.dma_start(ctx_list[:], offs2)
-        nc.sync.dma_start(c_sb[:, c_at[1] : c_at[1] + V], c_rows[1])
+        load_contexts(1)
         nc.sync.dma_start(tok_list[:], offs)
-        nc.sync.dma_start(x_sb[0][:], x_rows[0])
-        nc.sync.dma_start(x_sb[1][:], x_rows[1])
-        nc.sync.dma_start(c_sb[:, c_at[2] : c_at[2] + V], c_rows[2])
-        for r in range(4):
-            load_scale_rows(nc.sync, wsc_raw, 0, ws_scales, r)
-        nc.sync.dma_start(c_sb[:, c_at[3] : c_at[3] + V], c_rows[3])
-        nc.sync.dma_start(x_sb[2][:], x_rows[2])
-        nc.sync.dma_start(x_sb[3][:], x_rows[3])
-        for r in range(4):
-            load_scale_rows(nc.sync, wsc_raw, WA_ROW, wa_scales, r)
+        nc.sync.dma_start(x_sb[0][:], x_planes[0])
+        nc.sync.dma_start(x_sb[1][:], x_planes[1])
+        load_contexts(2)
+        load_scales(wsc_raw, 0, ws_scales)
+        load_contexts(3)
+        nc.sync.dma_start(x_sb[2][:], x_planes[2])
+        load_scales(wsc_raw, WA_ROW, wa_scales)
+        nc.sync.dma_start(x_sb[3][:], x_planes[3])
         nc.sync.dma_start(wa_raw[:], wa_words[0].rearrange("p n r -> p (n r)").bitcast(I32))
         nc.sync.dma_start(ws_raw[:], ws_words[0].rearrange("p n r -> p (n r)").bitcast(I32))
         nc.sync.dma_start(xs_sb[:].bitcast(I32), xs_words[0].bitcast(I32))
-        for r in range(4):
-            load_scale_rows(nc.sync, xs_sc, 0, xs_scales, r)
+        load_scales(xs_sc, 0, xs_scales)
 
         def deal(dst, src, run):
             nc.vector.tensor_copy(
-                dst[:].rearrange("p (t c i) -> p c t i", t=PACK, i=run),
-                src[:].rearrange("p (c i t) -> p c t i", t=PACK, i=run),
+                dst[:].rearrange("p (r c i) -> p c r i", r=PACK, i=run),
+                src[:].rearrange("p (c i r) -> p c r i", r=PACK, i=run),
             )
 
+        def slots(h):
+            return slice(h * HALF, (h + 1) * HALF)
+
         def entries(lst, h):
-            return lst[:, h * HALF // 16 : (h + 1) * HALF // 16]
+            return lst[:, h * HALF // LIST_ROWS : (h + 1) * HALF // LIST_ROWS]
 
-        summed = {(j, h): tile([P, HALF], F32, f"summed{j}{h}")[:] for j, h in ((2, 0), (3, 0), (3, 1))}
-        picked_all = {j: tile([P, J], F32, f"picked_all{j}") for j in (0, 1, 3)}
-        picked_2 = tile([P, HALF], F32, "picked_2")
-        picked = {(2, 0): picked_2[:], (2, 1): picked_all[3][:, 0:HALF], (3, 0): picked_all[3][:, 0:HALF], (3, 1): picked_all[3][:, HALF:J]}
-        summed_all = [tile([P, J], F32, f"summed_all{j}") for j in range(2)]
-        u_bf = sb.tile([P, J, PACK], BF16, name="u_bf", tag="u_bf", align_bytes=64)
-        summed[(2, 1)] = u_bf[:].rearrange("p c j -> p (c j)").bitcast(F32)[:, 0:HALF]
-        u_codes = {1: tile([P, HALF], I32, "u_codes1")}
-        u_sc = {1: tile([P, HALF], U8, "u_sc1")}
-        p_ps = [ps_p.tile([P, J], F32, name=f"p_ps{t}") for t in range(PACK)]
-        d_sb = [tile([P, J], F32, f"d{t}") for t in range(PACK)]
+        u_bf = tile([P, J, PACK], BF16, "u_bf")
+        u_codes = [tile([P, HALF], I32, f"u_codes{h}") for h in range(2)]
+        u_sc = [tile([P, HALF], U8, f"u_sc{h}") for h in range(2)]
+        freed = u_bf[:].rearrange("p j r -> p (j r)").bitcast(F32)[:, 0:HALF]
 
-        d_half = {(t, h): d_sb[t][:, h * HALF : (h + 1) * HALF] for t in range(2) for h in range(2)}
-        d_half[(1, 0)] = summed[(2, 1)]
+        picked_all = {r: tile([P, J], F32, f"picked_all{r}") for r in (0, 1, 3)}
+        picked = {(3, h): picked_all[3][:, slots(h)] for h in range(2)}
+        picked[(2, 0)] = tile([P, HALF], F32, "picked20")[:]
+        picked[(2, 1)] = picked[(3, 0)]
+        summed_all = [tile([P, J], F32, f"summed_all{r}") for r in range(2)]
+        summed = {(r, h): tile([P, HALF], F32, f"summed{r}{h}")[:] for r, h in ((2, 0), (3, 0), (3, 1))}
+        summed[(2, 1)] = freed
 
-        def pick_context(j, h):
-            nc.vector.tensor_copy(picked[(j, h)], c_sb[:, 0:V].indirect(entries(ctx_list, h)))
+        p_ps = [ps_p.tile([P, J], F32, name=f"p_ps{r}") for r in range(PACK)]
+        d_half = {(r, h): tile([P, HALF], F32, f"d{r}{h}")[:] for r, h in ((0, 0), (0, 1), (1, 1))}
+        d_half[(1, 0)] = freed
+        d_all = {r: tile([P, J], F32, f"d{r}") for r in (2, 3)}
 
-        def add_token(j, h):
-            nc.vector.tensor_tensor(summed[(j, h)], x_sb[j][:].indirect(entries(tok_list, h)), picked[(j, h)], ADD)
-            nc.scalar.activation(u_bf[:, h * HALF : (h + 1) * HALF, j], summed[(j, h)], COPY, scale=fk_sb[:, j : j + 1])
+        def pick_all_contexts(r):
+            nc.vector.tensor_copy(picked_all[r][:], c_sb[:, c_at[r] : c_at[r] + WIDE].indirect(ctx_list[:]))
+
+        def pick_contexts_2(h):
+            nc.vector.tensor_copy(picked[(2, h)], c_sb[:, c_at[2] : c_at[2] + V].indirect(entries(ctx_list, h)))
+
+        def add_tokens(r, token_entries, contexts, sums, cols):
+            nc.vector.tensor_tensor(sums, x_sb[r][:].indirect(token_entries), contexts, ADD)
+            nc.scalar.activation(u_bf[:, cols, r], sums, COPY, scale=fk_sb[:, r : r + 1])
+
+        def add_half(r, h):
+            add_tokens(r, entries(tok_list, h), picked[(r, h)], summed[(r, h)], slots(h))
 
         def expert(h):
-            cols = slice(h * HALF, (h + 1) * HALF)
-            nc.vector.quantize_mx(out=u_codes[h][:].bitcast(FP8X4), scales=u_sc[h][:], in_=u_bf[:, cols, :].rearrange("p c j -> p (c j)"))
-            for t in range(PACK):
-                m = slice(t * P, (t + 1) * P)
+            nc.vector.quantize_mx(
+                out=u_codes[h][:].bitcast(FP8X4), scales=u_sc[h][:], in_=u_bf[:, slots(h), :].rearrange("p j r -> p (j r)")
+            )
+            for r in range(PACK):
+                m = slice(r * P, (r + 1) * P)
                 nc.tensor.matmul_mx(
-                    out=p_ps[t][:, cols],
+                    out=p_ps[r][:, slots(h)],
                     lhsT=wa_dealt[:, m].bitcast(FP8X4),
                     lhsT_scale=wsc_dealt[WA_ROW:P, m],
                     rhs=u_codes[h][:].bitcast(FP8X4),
@@ -131,58 +152,56 @@ def tile_moe_expert_reads_token_and_context_pl_kernel(
                     stop=True,
                 )
 
-        def relu(t, h):
-            cols = slice(h * HALF, (h + 1) * HALF)
-            nc.scalar.activation(d_half[(t, h)], p_ps[t][:, cols], RELU)
+        def relu_half(r, h):
+            nc.scalar.activation(d_half[(r, h)], p_ps[r][:, slots(h)], RELU)
 
-        def scatter(t, h):
-            nc.vector.tensor_copy(dp[t][:].indirect(entries(tok_list, h)), d_half[(t, h)])
+        def scatter_half(r, h):
+            nc.vector.tensor_copy(dp[r][:].indirect(entries(tok_list, h)), d_half[(r, h)])
 
-        for j in (0, 1):
-            nc.vector.tensor_copy(picked_all[j][:], c_sb[:, c_at[j] : c_at[j] + WIDE].indirect(ctx_list[:]))
-        for j in (0, 1):
-            nc.vector.tensor_tensor(summed_all[j][:], x_sb[j][:].indirect(tok_list[:]), picked_all[j][:], ADD)
-            nc.scalar.activation(u_bf[:, :, j], summed_all[j][:], COPY, scale=fk_sb[:, j : j + 1])
-        pick_context(2, 0)
-        nc.vector.tensor_copy(picked_all[3][:], c_sb[:, V : V + WIDE].indirect(ctx_list[:]))
-        add_token(2, 0)
-        add_token(3, 0)
-        add_token(3, 1)
-        pick_context(2, 1)
+        for r in (0, 1):
+            pick_all_contexts(r)
+        for r in (0, 1):
+            add_tokens(r, tok_list[:], picked_all[r][:], summed_all[r][:], slice(0, J))
+        pick_contexts_2(0)
+        pick_all_contexts(3)
+        add_half(2, 0)
         deal(wsc_dealt, wsc_raw, 16)
+        add_half(3, 0)
+        add_half(3, 1)
+        pick_contexts_2(1)
         deal(wa_dealt, wa_raw, 4)
-        u_codes[0] = sb.tile([P, HALF], I32, name="u_codes0", tag="wa_raw", align_bytes=64)
-        u_sc[0] = sb.tile([P, HALF], U8, name="u_sc0", tag="wsc_raw", align_bytes=64)
         expert(0)
-        relu(0, 0)
+        relu_half(0, 0)
         deal(ws_dealt, ws_raw, 4)
-        add_token(2, 1)
-        scatter(0, 0)
-        relu(1, 0)
+        add_half(2, 1)
+        scatter_half(0, 0)
+        relu_half(1, 0)
         expert(1)
-        relu(0, 1)
-        relu(1, 1)
-        for t in (2, 3):
-            nc.scalar.activation(d_sb[t][:], p_ps[t][:], RELU)
-        scatter(1, 0)
-        scatter(0, 1)
-        scatter(1, 1)
-        for t, tag in ((2, "x2"), (3, "u_bf")):
-            dp.append(sb.tile([P, T], F32, name=f"dp{t}", tag=tag, align_bytes=64))
-            nc.gpsimd.memset(dp[t][:], 0.0)
-            nc.vector.tensor_copy(dp[t][:].indirect(tok_list[:]), d_sb[t][:])
+        relu_half(0, 1)
+        relu_half(1, 1)
+        for r in (2, 3):
+            nc.scalar.activation(d_all[r][:], p_ps[r][:], RELU)
+        scatter_half(1, 0)
+        scatter_half(0, 1)
+        scatter_half(1, 1)
+        for r, tag in ((2, "x2"), (3, "u_bf")):
+            dp.append(tile([P, T], F32, f"dp{r}", tag))
+            nc.gpsimd.memset(dp[r][:], 0.0)
+            nc.vector.tensor_copy(dp[r][:].indirect(tok_list[:]), d_all[r][:])
 
         y_pair = [tile([P, 2, T], F32, f"y_pair{a}") for a in range(2)]
-        z_sb = [tile([P, T], F32, f"z{t}")[:] for t in range(2)] + [y_pair[1][:, 1, :]]
-        z_end = tile([P, 256], F32, "z_end")
+        last = PACK - 1
+        y_last = y_pair[1][:, 1, :]
+        z_sb = [tile([P, T], F32, f"z{r}")[:] for r in range(2)] + [y_last]
+        z_end = tile([P, T - POOL_FROM], F32, "z_end")
         y_bf = tile([P, T, PACK], BF16, "y_bf")
         y_codes = tile([P, T], I32, "y_codes")
         y_sc = tile([P, T], U8, "y_sc")
-        y_rows = out_0.rearrange("(p t) c -> t p c", t=PACK)
-        words_out = out_1[0].rearrange("p c r -> p (c r)").bitcast(I32)
+        y_planes = out_0.rearrange("(p r) t -> r p t", r=PACK)
+        words_out = out_1[0].rearrange("p t r -> p (t r)").bitcast(I32)
 
-        def shared(t, g):
-            m = slice(t * P, (t + 1) * P)
+        def shared(r, g):
+            m = slice(r * P, (r + 1) * P)
             z_ps = ps_z.tile([P, BANK], F32, name="z_ps")
             nc.tensor.matmul_mx(
                 out=z_ps[:],
@@ -195,43 +214,43 @@ def tile_moe_expert_reads_token_and_context_pl_kernel(
             )
             return z_ps
 
-        def rounded(a, lo, hi):
-            return y_bf[:, lo:hi, 2 * a : 2 * a + 2], y_pair[a][:, :, lo:hi].rearrange("p t c -> p c t")
+        def round_pair_on_scalar(a, lo, hi):
+            nc.scalar.copy(y_bf[:, lo:hi, 2 * a : 2 * a + 2], y_pair[a][:, :, lo:hi].rearrange("p b t -> p t b"))
 
-        for t in range(PACK - 1):
-            y_t = y_pair[t // 2][:, t % 2, :]
-            for g in range(2):
+        for r in range(last):
+            y_r = y_pair[r // 2][:, r % 2, :]
+            for g in range(T // BANK):
                 cols = slice(g * BANK, (g + 1) * BANK)
-                nc.scalar.copy(z_sb[t][:, cols], shared(t, g)[:])
-                nc.gpsimd.tensor_tensor(y_t[:, cols], z_sb[t][:, cols], dp[t][:, cols], ADD)
-            nc.sync.dma_start(y_rows[t], y_t)
+                nc.scalar.copy(z_sb[r][:, cols], shared(r, g)[:])
+                nc.gpsimd.tensor_tensor(y_r[:, cols], z_sb[r][:, cols], dp[r][:, cols], ADD)
+            nc.sync.dma_start(y_planes[r], y_r)
 
-        last = PACK - 1
-        z_last = [shared(last, g) for g in range(2)]
-        nc.scalar.copy(z_end[:], z_last[1][:, 256:BANK])
-        for g in range(2):
-            nc.scalar.copy(*rounded(0, g * BANK, (g + 1) * BANK))
-        y_last = y_pair[1][:, 1, :]
-        for lo, hi in ((0, 256), (512, 768), (256, 512)):
+        z_last = [shared(last, g) for g in range(T // BANK)]
+        nc.scalar.copy(z_end[:], z_last[1][:, POOL_FROM - BANK : BANK])
+        for g in range(T // BANK):
+            round_pair_on_scalar(0, g * BANK, (g + 1) * BANK)
+
+        for lo, hi in ((0, QUARTER), (VECTOR_FROM, POOL_FROM), (QUARTER, BANK), (BANK, VECTOR_FROM)):
             g = lo // BANK
             nc.vector.tensor_tensor(y_last[:, lo:hi], z_last[g][:, lo - g * BANK : hi - g * BANK], dp[last][:, lo:hi], ADD)
-        nc.gpsimd.tensor_tensor(y_last[:, 768:T], z_end[:], dp[last][:, 768:T], ADD)
-        for g in range(2):
-            nc.sync.dma_start(y_rows[last][:, g * BANK : (g + 1) * BANK], y_last[:, g * BANK : (g + 1) * BANK])
-        for lo, hi in ((0, 256), (256, 512)):
-            nc.scalar.copy(*rounded(1, lo, hi))
+        nc.gpsimd.tensor_tensor(y_last[:, POOL_FROM:T], z_end[:], dp[last][:, POOL_FROM:T], ADD)
+        for g in range(T // BANK):
+            cols = slice(g * BANK, (g + 1) * BANK)
+            nc.sync.dma_start(y_planes[last][:, cols], y_last[:, cols])
+        for lo, hi in ((0, QUARTER), (QUARTER, BANK), (BANK, VECTOR_FROM)):
+            round_pair_on_scalar(1, lo, hi)
         nc.vector.tensor_copy(
-            y_bf[:, 512:T, 2:4].rearrange("p (c i) t -> p c t i", i=4),
-            y_pair[1][:, :, 512:T].rearrange("p t (c i) -> p c t i", i=4),
+            y_bf[:, VECTOR_FROM:T, 2:PACK].rearrange("p (c i) b -> p c b i", i=4),
+            y_pair[1][:, :, VECTOR_FROM:T].rearrange("p b (c i) -> p c b i", i=4),
         )
-        for lo, hi in ((0, 256), (768, T), (512, 768), (256, 512)):
+
+        for quarter in (0, 3, 1, 2):
+            cols = slice(quarter * QUARTER, (quarter + 1) * QUARTER)
             nc.vector.quantize_mx(
-                out=y_codes[:, lo:hi].bitcast(FP8X4),
-                scales=y_sc[:, lo:hi],
-                in_=y_bf[:, lo:hi, :].rearrange("p c t -> p (c t)"),
+                out=y_codes[:, cols].bitcast(FP8X4), scales=y_sc[:, cols], in_=y_bf[:, cols, :].rearrange("p t r -> p (t r)")
             )
-            nc.sync.dma_start(words_out[:, lo:hi], y_codes[:, lo:hi])
-        sc_rows = out_2[0].bitcast(I32).rearrange("(q r) c -> r q c", r=4)
-        for r in range(4):
-            eng = nc.scalar if r % 2 else nc.sync
-            eng.dma_start(sc_rows[r], y_sc[:].bitcast(I32)[r:P:32, :])
+            nc.sync.dma_start(words_out[:, cols], y_codes[:, cols])
+        scale_rows = out_2[0].bitcast(I32).rearrange("(q i) t -> i q t", i=4)
+        for i in range(4):
+            queue = nc.scalar if i % 2 else nc.sync
+            queue.dma_start(scale_rows[i], y_sc[:].bitcast(I32)[i:P:QUADRANT, :])

from contextlib import ExitStack

import concourse.mybir as mybir

K, T, V, J, L, N = 512, 1024, 512, 512, 512, 512
FLOPS = 2 * K * N * J + 2 * L * N * T

F32 = mybir.dt.float32
BF16 = mybir.dt.bfloat16
I32 = mybir.dt.int32
U16 = mybir.dt.uint16
U8 = mybir.dt.uint8
FP8X4 = mybir.dt.float8_e4m3fn_x4
FP4X4 = mybir.dt.float4_e2m1fn_x4
ADD = mybir.AluOpType.add
COPY = mybir.ActivationFunctionType.Copy
RELU = mybir.ActivationFunctionType.Relu

P = 128
PACK = 4
LIST_ROWS = 16
HALF = J // 2
BANK = 512
Z_BANKS = 4
QUADRANT = 32
WA_ROW = 4
WIDE = 704
QUARTER = T // 4
POOL_FROM = 3 * QUARTER
VECTOR_FROM = 640


def tile_moe_expert_reads_token_and_context_pl_kernel(
    tc, xf, cx, fk, wa_words, wa_scales, xs_words, xs_scales, ws_words, ws_scales, offs, offs2, out_0, out_1, out_2
):
    nc = tc.nc
    with ExitStack() as ctx:
        sb = ctx.enter_context(tc.tile_pool(name="sb", bufs=1))
        ps_p = ctx.enter_context(tc.psum_pool(name="ps_p", bufs=1))
        ps_z = ctx.enter_context(tc.psum_pool(name="ps_z", bufs=Z_BANKS))

        def tile(shape, dtype, name, tag=None):
            return sb.tile(shape, dtype, name=name, tag=tag or name, align_bytes=64)

        tok_list = sb.tile([P, J // LIST_ROWS], U16, name="tok_list")
        ctx_list = sb.tile([P, J // LIST_ROWS], U16, name="ctx_list")
        x_sb = [tile([P, T], F32, f"x{r}") for r in range(PACK)]
        c_sb = tile([P, 3 * V + WIDE], F32, "c_sb")
        c_at = (3 * V, 2 * V, 0, V)
        fk_sb = tile([P, PACK], F32, "fk_sb")
        wa_raw = tile([P, N], I32, "wa_raw")
        ws_raw = tile([P, N], I32, "ws_raw")
        wsc_raw = tile([P, N], U8, "wsc_raw")
        wa_dealt = tile([P, N], I32, "wa_dealt")
        ws_dealt = tile([P, N], I32, "ws_dealt")
        wsc_dealt = tile([P, N], U8, "wsc_dealt")
        xs_sb = tile([P, 2 * T], U8, "xs_sb")
        xs_sc = tile([P, T], U8, "xs_sc")
        dp = [tile([P, T], F32, f"dp{r}") for r in range(2)]

        nc.gpsimd.memset(wsc_raw[:].bitcast(I32), 0)
        nc.vector.memset(c_sb[:, PACK * V : 3 * V + WIDE], 0.0)
        nc.vector.memset(xs_sc[:].bitcast(I32), 0)
        for r in range(2):
            nc.gpsimd.memset(dp[r][:], 0.0)

        x_planes = xf.rearrange("(p r) t -> r p t", r=PACK)
        c_planes = cx.rearrange("(p r) v -> r p v", r=PACK)

        def load_contexts(r):
            nc.sync.dma_start(c_sb[:, c_at[r] : c_at[r] + V], c_planes[r])

        def load_scales(plane, first, scales):
            for q in range(P // QUADRANT):
                at = QUADRANT * q + first
                nc.sync.dma_start(plane[:].bitcast(I32)[at : at + 4, :], scales[0].bitcast(I32)[4 * q : 4 * q + 4, :])

        nc.scalar.dma_start(fk_sb[:], fk.rearrange("(p r) o -> p (r o)", r=PACK))
        load_contexts(0)
        nc.sync.dma_start(ctx_list[:], offs2)
        load_contexts(1)
        nc.sync.dma_start(tok_list[:], offs)
        nc.sync.dma_start(x_sb[0][:], x_planes[0])
        nc.sync.dma_start(x_sb[1][:], x_planes[1])
        load_contexts(2)
        load_scales(wsc_raw, 0, ws_scales)
        load_contexts(3)
        nc.sync.dma_start(x_sb[2][:], x_planes[2])
        load_scales(wsc_raw, WA_ROW, wa_scales)
        nc.sync.dma_start(x_sb[3][:], x_planes[3])
        nc.sync.dma_start(wa_raw[:], wa_words[0].rearrange("p n r -> p (n r)").bitcast(I32))
        nc.sync.dma_start(ws_raw[:], ws_words[0].rearrange("p n r -> p (n r)").bitcast(I32))
        nc.sync.dma_start(xs_sb[:].bitcast(I32), xs_words[0].bitcast(I32))
        load_scales(xs_sc, 0, xs_scales)

        def deal(dst, src, run):
            nc.vector.tensor_copy(
                dst[:].rearrange("p (r c i) -> p c r i", r=PACK, i=run),
                src[:].rearrange("p (c i r) -> p c r i", r=PACK, i=run),
            )

        def slots(h):
            return slice(h * HALF, (h + 1) * HALF)

        def entries(lst, h):
            return lst[:, h * HALF // LIST_ROWS : (h + 1) * HALF // LIST_ROWS]

        u_bf = tile([P, J, PACK], BF16, "u_bf")
        u_codes = [tile([P, HALF], I32, f"u_codes{h}") for h in range(2)]
        u_sc = [tile([P, HALF], U8, f"u_sc{h}") for h in range(2)]
        freed = u_bf[:].rearrange("p j r -> p (j r)").bitcast(F32)[:, 0:HALF]

        picked_all = {r: tile([P, J], F32, f"picked_all{r}") for r in (0, 1, 3)}
        picked = {(3, h): picked_all[3][:, slots(h)] for h in range(2)}
        picked[(2, 0)] = tile([P, HALF], F32, "picked20")[:]
        picked[(2, 1)] = picked[(3, 0)]
        summed_all = [tile([P, J], F32, f"summed_all{r}") for r in range(2)]
        summed = {(r, h): tile([P, HALF], F32, f"summed{r}{h}")[:] for r, h in ((2, 0), (3, 0), (3, 1))}
        summed[(2, 1)] = freed

        p_ps = [ps_p.tile([P, J], F32, name=f"p_ps{r}") for r in range(PACK)]
        d_half = {(r, h): tile([P, HALF], F32, f"d{r}{h}")[:] for r, h in ((0, 0), (0, 1), (1, 1))}
        d_half[(1, 0)] = freed
        d_all = {r: tile([P, J], F32, f"d{r}") for r in (2, 3)}

        def pick_all_contexts(r):
            nc.vector.tensor_copy(picked_all[r][:], c_sb[:, c_at[r] : c_at[r] + WIDE].indirect(ctx_list[:]))

        def pick_contexts_2(h):
            nc.vector.tensor_copy(picked[(2, h)], c_sb[:, c_at[2] : c_at[2] + V].indirect(entries(ctx_list, h)))

        def add_tokens(r, token_entries, contexts, sums, cols):
            nc.vector.tensor_tensor(sums, x_sb[r][:].indirect(token_entries), contexts, ADD)
            nc.scalar.activation(u_bf[:, cols, r], sums, COPY, scale=fk_sb[:, r : r + 1])

        def add_half(r, h):
            add_tokens(r, entries(tok_list, h), picked[(r, h)], summed[(r, h)], slots(h))

        def expert(h):
            nc.vector.quantize_mx(
                out=u_codes[h][:].bitcast(FP8X4), scales=u_sc[h][:], in_=u_bf[:, slots(h), :].rearrange("p j r -> p (j r)")
            )
            for r in range(PACK):
                m = slice(r * P, (r + 1) * P)
                nc.tensor.matmul_mx(
                    out=p_ps[r][:, slots(h)],
                    lhsT=wa_dealt[:, m].bitcast(FP8X4),
                    lhsT_scale=wsc_dealt[WA_ROW:P, m],
                    rhs=u_codes[h][:].bitcast(FP8X4),
                    rhs_scale=u_sc[h][:],
                    start=True,
                    stop=True,
                )

        def relu_half(r, h):
            nc.scalar.activation(d_half[(r, h)], p_ps[r][:, slots(h)], RELU)

        def scatter_half(r, h):
            nc.vector.tensor_copy(dp[r][:].indirect(entries(tok_list, h)), d_half[(r, h)])

        for r in (0, 1):
            pick_all_contexts(r)
        for r in (0, 1):
            add_tokens(r, tok_list[:], picked_all[r][:], summed_all[r][:], slice(0, J))
        pick_contexts_2(0)
        pick_all_contexts(3)
        add_half(2, 0)
        deal(wsc_dealt, wsc_raw, 16)
        add_half(3, 0)
        add_half(3, 1)
        pick_contexts_2(1)
        deal(wa_dealt, wa_raw, 4)
        expert(0)
        relu_half(0, 0)
        deal(ws_dealt, ws_raw, 4)
        add_half(2, 1)
        scatter_half(0, 0)
        relu_half(1, 0)
        expert(1)
        relu_half(0, 1)
        relu_half(1, 1)
        for r in (2, 3):
            nc.scalar.activation(d_all[r][:], p_ps[r][:], RELU)
        scatter_half(1, 0)
        scatter_half(0, 1)
        scatter_half(1, 1)
        for r, tag in ((2, "x2"), (3, "u_bf")):
            dp.append(tile([P, T], F32, f"dp{r}", tag))
            nc.gpsimd.memset(dp[r][:], 0.0)
            nc.vector.tensor_copy(dp[r][:].indirect(tok_list[:]), d_all[r][:])

        y_pair = [tile([P, 2, T], F32, f"y_pair{a}") for a in range(2)]
        last = PACK - 1
        y_last = y_pair[1][:, 1, :]
        z_sb = [tile([P, T], F32, f"z{r}")[:] for r in range(2)] + [y_last]
        z_end = tile([P, T - POOL_FROM], F32, "z_end")
        y_bf = tile([P, T, PACK], BF16, "y_bf")
        y_codes = tile([P, T], I32, "y_codes")
        y_sc = tile([P, T], U8, "y_sc")
        y_planes = out_0.rearrange("(p r) t -> r p t", r=PACK)
        words_out = out_1[0].rearrange("p t r -> p (t r)").bitcast(I32)

        def shared(r, g):
            m = slice(r * P, (r + 1) * P)
            z_ps = ps_z.tile([P, BANK], F32, name="z_ps")
            nc.tensor.matmul_mx(
                out=z_ps[:],
                lhsT=ws_dealt[:, m].bitcast(FP8X4),
                lhsT_scale=wsc_dealt[:, m],
                rhs=xs_sb[:, 2 * g * BANK : 2 * (g + 1) * BANK].bitcast(FP4X4),
                rhs_scale=xs_sc[:, g * BANK : (g + 1) * BANK],
                start=True,
                stop=True,
            )
            return z_ps

        def round_pair_on_scalar(a, lo, hi):
            nc.scalar.copy(y_bf[:, lo:hi, 2 * a : 2 * a + 2], y_pair[a][:, :, lo:hi].rearrange("p b t -> p t b"))

        for r in range(last):
            y_r = y_pair[r // 2][:, r % 2, :]
            for g in range(T // BANK):
                cols = slice(g * BANK, (g + 1) * BANK)
                nc.scalar.copy(z_sb[r][:, cols], shared(r, g)[:])
                nc.gpsimd.tensor_tensor(y_r[:, cols], z_sb[r][:, cols], dp[r][:, cols], ADD)
            nc.sync.dma_start(y_planes[r], y_r)

        z_last = [shared(last, g) for g in range(T // BANK)]
        nc.scalar.copy(z_end[:], z_last[1][:, POOL_FROM - BANK : BANK])
        for g in range(T // BANK):
            round_pair_on_scalar(0, g * BANK, (g + 1) * BANK)

        for lo, hi in ((0, QUARTER), (VECTOR_FROM, POOL_FROM), (QUARTER, BANK), (BANK, VECTOR_FROM)):
            g = lo // BANK
            nc.vector.tensor_tensor(y_last[:, lo:hi], z_last[g][:, lo - g * BANK : hi - g * BANK], dp[last][:, lo:hi], ADD)
        nc.gpsimd.tensor_tensor(y_last[:, POOL_FROM:T], z_end[:], dp[last][:, POOL_FROM:T], ADD)
        for g in range(T // BANK):
            cols = slice(g * BANK, (g + 1) * BANK)
            nc.sync.dma_start(y_planes[last][:, cols], y_last[:, cols])
        for lo, hi in ((0, QUARTER), (QUARTER, BANK), (BANK, VECTOR_FROM)):
            round_pair_on_scalar(1, lo, hi)
        nc.vector.tensor_copy(
            y_bf[:, VECTOR_FROM:T, 2:PACK].rearrange("p (c i) b -> p c b i", i=4),
            y_pair[1][:, :, VECTOR_FROM:T].rearrange("p b (c i) -> p c b i", i=4),
        )

        for quarter in (0, 3, 1, 2):
            cols = slice(quarter * QUARTER, (quarter + 1) * QUARTER)
            nc.vector.quantize_mx(
                out=y_codes[:, cols].bitcast(FP8X4), scales=y_sc[:, cols], in_=y_bf[:, cols, :].rearrange("p t r -> p (t r)")
            )
            nc.sync.dma_start(words_out[:, cols], y_codes[:, cols])
        scale_rows = out_2[0].bitcast(I32).rearrange("(q i) t -> i q t", i=4)
        for i in range(4):
            queue = nc.scalar if i % 2 else nc.sync
            queue.dma_start(scale_rows[i], y_sc[:].bitcast(I32)[i:P:QUADRANT, :])
